import numpy as np
import ml_dtypes


def mxq(x, axis, fmt="e4m3"):
    dtype, down = {"e4m3": (ml_dtypes.float8_e4m3fn, 7), "e5m2": (ml_dtypes.float8_e5m2, 14)}[fmt]
    v = np.moveaxis(np.asarray(x, np.float32).astype(ml_dtypes.bfloat16).astype(np.float64), axis, -1)
    blocks = v.reshape(v.shape[:-1] + (-1, 32))
    amax = np.abs(blocks).max(-1, keepdims=True)
    byte = np.maximum(np.where(amax > 0, np.frexp(amax)[1] - 1 + 127, 0) - down, 1)
    scale = np.exp2(byte - 127.0)
    codes = (blocks / scale).astype(np.float32).astype(dtype).astype(np.float64)
    return np.moveaxis((codes * scale).reshape(v.shape), -1, axis)


WIDE = False


def mx_kscale(k):
    if not WIDE:
        return np.ones(k)
    levels = np.array([10, -10, 5, -5, 0])
    if k % 512:
        return np.exp2(np.random.permutation(np.resize(levels, k // 32))).repeat(32)
    a = np.empty((k // 512, 16))
    for p in range(k // 512):
        a[p, :8] = np.random.permutation(np.resize(levels, 8))
        for g in range(8):
            far = levels[np.abs(levels - a[p, g]) >= 10]
            a[p, g + 8] = far[np.random.randint(len(far))]
    return np.exp2(a.ravel()).repeat(32)


def f64(x):
    return np.asarray(x).astype(np.float64)


def striped(idx):
    return np.tile(idx.reshape(-1, 16).T, (8, 1)).astype(np.uint16)


def unstriped(offs):
    return offs[:16].T.reshape(-1).astype(np.int64)


E2M1 = np.array([0.0, 0.5, 1.0, 1.5, 2.0, 3.0, 4.0, 6.0, -0.0, -0.5, -1.0, -1.5, -2.0, -3.0, -4.0, -6.0])


def pack_weight(w, fmt):
    k, n = w.shape
    w = f64(np.asarray(w, np.float32).astype(ml_dtypes.bfloat16)).reshape(k // 32, 32, n)
    amax = np.abs(w).max(1)
    if fmt == "e4m3":
        byte = np.frexp(amax)[1] - 1 + 127 - 7
    else:
        mant, ex = np.frexp(amax / 6.0)
        byte = np.where(mant > 0.5, ex, ex - 1) + 127
    byte = np.clip(np.where(amax > 0, byte, 1), 1, 254)
    scaled = (w * np.exp2(127.0 - byte)[:, None, :]).reshape(k, n).astype(np.float32)
    by_word = np.ascontiguousarray(scaled.reshape(k // 512, 128, 4, n).transpose(0, 1, 3, 2))
    if fmt == "e4m3":
        words = by_word.astype(ml_dtypes.float8_e4m3fn).view(np.uint8)
    else:
        c = by_word.astype(ml_dtypes.float4_e2m1fn).view(np.uint8) & 0xF
        words = (c[..., 0::2] | (c[..., 1::2] << 4)).reshape(k // 512, 128, 2 * n)
    return np.ascontiguousarray(words), np.ascontiguousarray(byte.astype(np.uint8).reshape(k // 512, 16, n))


def unpack_weight(words, scales, fmt):
    g, _, n = scales.shape
    words = np.ascontiguousarray(words).reshape(g, 128, n, -1)
    if fmt == "e4m3":
        vals = words.view(ml_dtypes.float8_e4m3fn).astype(np.float64)
    else:
        nib = np.empty((g, 128, n, 4), np.uint8)
        nib[..., 0::2] = words & 0xF
        nib[..., 1::2] = words >> 4
        vals = E2M1[nib]
    vals = vals * np.repeat(np.exp2(scales.astype(np.float64) - 127.0), 8, axis=1)[..., None]
    return vals.transpose(0, 1, 3, 2).reshape(g * 512, n)


def gelu(v):
    return 0.5 * v * (1.0 + np.tanh(np.sqrt(2.0 / np.pi) * (v + 0.044715 * v**3)))


def striped8(idx):
    return np.concatenate([v.reshape(-1, 16).T for v in idx]).astype(np.uint16)


def unstriped8(offs):
    return np.stack([offs[16 * g:16 * g + 16].T.reshape(-1) for g in range(8)]).astype(np.int64)


def heads(xT, wgt, idx8):
    k = np.arange(xT.shape[0])
    return wgt[k // 4 % 128] * xT[k[:, None], idx8[k % 512 // 64]]


K, T, S, H, N = 1536, 2048, 1024, 1024, 512

def setup_inputs():
    n = np.random.standard_normal
    s = mx_kscale(K)[:, None]
    u = mx_kscale(H)[:, None]
    xT = (n((K, T)) * s).astype(np.float32)
    wgt = np.repeat(np.random.uniform(0.5, 2.0, (8, S)), 16, axis=0).astype(np.float32)
    offs = striped8(np.stack([np.random.permutation(T)[:S] for _ in range(8)]))
    w1 = (n((K, H)) / np.sqrt(K) / s).astype(np.float32)
    b1 = (0.5 * n(H)).astype(np.float32)
    gain = (np.exp(0.3 * n(H)) * u[:, 0]).astype(np.float32)
    w2_words, w2_scales = pack_weight(n((H, N)) / np.sqrt(H) / u, "e2m1")
    return {"xT": xT, "wgt": wgt, "offs": offs, "w1": w1, "b1": b1, "gain": gain,
            "w2_words": w2_words, "w2_scales": w2_scales}

def reference(xT, wgt, offs, w1, b1, gain, w2_words, w2_scales):
    xg = heads(f64(xT), f64(wgt), unstriped8(offs))
    xq = mxq(xg, 0, "e4m3")
    w1q = mxq(f64(w1), 0, "e4m3")
    f = w1q.T @ xq
    e = np.exp(f + f64(b1)[:, None])
    h = f64(gain)[:, None] * np.log(1.0 + e)
    hq = mxq(h, 0, "e4m3")
    w2 = unpack_weight(w2_words, w2_scales, "e2m1")
    return w2.T @ hq

@@ -1,0 +1,214 @@
+from contextlib import ExitStack
+
+import concourse.mybir as mybir
+
+K, T, S, H, N = 1536, 2048, 1024, 1024, 512
+FLOPS = 2 * K * H * S + 2 * H * N * S
+
+F32 = mybir.dt.float32
+BF16 = mybir.dt.bfloat16
+I32 = mybir.dt.int32
+U32 = mybir.dt.uint32
+U16 = mybir.dt.uint16
+U8 = mybir.dt.uint8
+FP8X4 = mybir.dt.float8_e4m3fn_x4
+FP4X4 = mybir.dt.float4_e2m1fn_x4
+ALU = mybir.AluOpType
+ACT = mybir.ActivationFunctionType
+
+P = 128
+PACK = 4
+K_PASS = P * PACK
+COLS = 512
+RUN = 4
+PASSES_1 = K // K_PASS
+PASSES_2 = H // K_PASS
+HALVES = S // COLS
+TINY = 2.0**-60
+
+
+def tile_list_book_intensity_risk_kernel(tc, xT, wgt, offs, w1, b1, gain, w2_words, w2_scales, out):
+    nc = tc.nc
+    with ExitStack() as ctx:
+        keep = ctx.enter_context(tc.tile_pool(name="keep", bufs=1))
+        ring = ctx.enter_context(tc.tile_pool(name="ring", bufs=2))
+        psum = ctx.enter_context(tc.psum_pool(name="psum", bufs=1))
+
+        offsets = keep.tile([P, S // 16], U16, name="offsets")
+        nc.sync.dma_start(offsets[:], offs)
+
+        warm = keep.tile([P, 2], F32, name="warm")
+        nc.gpsimd.memset(warm[:, 0:1], 0.0)
+        nc.scalar.activation(warm[:, 1:2], warm[:, 0:1], ACT.Sigmoid)
+
+        bias = keep.tile([P, PASSES_2, PACK], F32, name="bias")
+        nc.gpsimd.dma_start(bias[:], b1.rearrange("(b p t) -> p b t", p=P, t=PACK))
+        gains = keep.tile([P, PASSES_2, PACK], F32, name="gains")
+        nc.gpsimd.dma_start(gains[:], gain.rearrange("(b p t) -> p b t", p=P, t=PACK))
+        neg_bias = keep.tile([P, PASSES_2, PACK], F32, name="neg_bias")
+        nc.gpsimd.tensor_scalar(neg_bias[:], bias[:], -1.0, 0.0, ALU.mult, ALU.add)
+        neg_gains = keep.tile([P, PASSES_2, PACK], F32, name="neg_gains")
+        nc.gpsimd.tensor_scalar(neg_gains[:], gains[:], -1.0, 0.0, ALU.mult, ALU.add)
+        w2_scale = keep.tile([P, PASSES_2 * N], U8, name="w2_scale", align_bytes=64)
+        nc.gpsimd.memset(w2_scale[:].bitcast(I32), 0)
+
+        weights = [keep.tile([P, COLS], F32, name=f"weights{h}") for h in range(HALVES)]
+        planes = {}
+        w1_raw = {}
+
+        def load_plane(a, i):
+            planes[a, i] = ring.tile([P, T], F32, name="plane", tag="big", bufs=10)
+            rows = xT[a * K_PASS : (a + 1) * K_PASS, :].rearrange("(p i) t -> p i t", i=PACK)
+            nc.sync.dma_start(planes[a, i][:], rows[:, i, :])
+
+        def load_w1(a, b):
+            w1_raw[a, b] = ring.tile([P, PACK, K_PASS], F32, name="w1_raw", bufs=3)
+            rows = w1[a * K_PASS : (a + 1) * K_PASS, b * K_PASS : (b + 1) * K_PASS]
+            nc.sync.dma_start(w1_raw[a, b][:], rows.rearrange("(p i) r -> p i r", i=PACK))
+
+        nc.sync.dma_start(weights[0][:], wgt[:, 0:COLS])
+        load_plane(0, 0)
+        nc.sync.dma_start(weights[1][:], wgt[:, COLS:S])
+        for a in range(PASSES_1):
+            for i in range(PACK):
+                if (a, i) != (0, 0):
+                    load_plane(a, i)
+                if i == 1:
+                    load_w1(a, 0)
+        for a in range(PASSES_1):
+            load_w1(a, 1)
+
+        w2_code = keep.tile([P, PASSES_2, 2 * N], U8, name="w2_code", align_bytes=64)
+        nc.sync.dma_start(w2_code[:].bitcast(I32), w2_words.rearrange("b p c -> p b c").bitcast(I32))
+        for q in range(4):
+            nc.sync.dma_start(
+                w2_scale[32 * q : 32 * q + 4, :].rearrange("p (b n) -> p b n", b=PASSES_2).bitcast(I32),
+                w2_scales[:, 4 * q : 4 * q + 4, :].rearrange("b r n -> r b n").bitcast(I32),
+            )
+
+        def quantize(grouped, name, cols=COLS):
+            codes = keep.tile([P, cols], U32, name=name + "_codes", align_bytes=64)
+            scales = keep.tile([P, cols], U8, name=name + "_scales", align_bytes=64)
+            nc.vector.quantize_mx(out=codes[:].bitcast(FP8X4), scales=scales[:], in_=grouped[:])
+            return codes, scales
+
+        def by_runs_out(grouped):
+            return grouped[:].rearrange("p (c i t) -> p c t i", i=RUN, t=PACK)
+
+        def by_runs_in(four):
+            return four.rearrange("p t (c i) -> p c t i", i=RUN)
+
+        def group_w1(a, b, on_scalar):
+            if on_scalar:
+                grouped = ring.tile([P, PACK * K_PASS], BF16, name="w1_grouped", bufs=1, align_bytes=64)
+            else:
+                grouped = ring.tile([P, PACK * K_PASS], BF16, name="w1_late", tag=f"late{a % 2}", bufs=1, align_bytes=64)
+            dst = grouped[:].rearrange("p (t m i) -> p m i t", t=PACK, i=PACK)
+            src = w1_raw[a, b][:].rearrange("p i (m t) -> p m i t", t=PACK)
+            if on_scalar:
+                nc.scalar.copy(dst, src)
+            else:
+                nc.vector.tensor_copy(dst, src)
+            return grouped
+
+        w1_q = {}
+        x_q = {}
+        banks = {}
+
+        def first_product(a, b, h):
+            for t in range(PACK):
+                if a == 0:
+                    banks[h, t] = psum.tile([P, COLS], F32, name=f"bank{h}{t}")
+                w_codes, w_scales = w1_q[a, b]
+                x_codes, x_scales = x_q[a, h]
+                nc.tensor.matmul_mx(
+                    out=banks[h, t][:],
+                    lhsT=w_codes[:, t * P : (t + 1) * P].bitcast(FP8X4),
+                    lhsT_scale=w_scales[:, t * P : (t + 1) * P],
+                    rhs=x_codes[:].bitcast(FP8X4),
+                    rhs_scale=x_scales[:],
+                    start=(a == 0),
+                    stop=(a == PASSES_1 - 1),
+                )
+
+        for a in range(PASSES_1):
+            picked = [ring.tile([P, PACK, COLS], F32, name="picked", bufs=4) for h in range(HALVES)]
+            for i in range(PACK):
+                for h in range(HALVES):
+                    lists = offsets[:, h * COLS // 16 : (h + 1) * COLS // 16]
+                    nc.vector.tensor_tensor(picked[h][:, i, :], planes[a, i][:].indirect(lists), weights[h][:], ALU.mult)
+                if i == 1:
+                    w_grouped = group_w1(a, 0, True)
+                if i == 2:
+                    w1_q[a, 0] = quantize(w_grouped, f"w1_{a}0")
+            for h in range(HALVES):
+                grouped = ring.tile([P, PACK * COLS], BF16, name="x_grouped", tag=f"late{h}", bufs=1, align_bytes=64)
+                if (a, h) == (PASSES_1 - 1, HALVES - 1):
+                    nc.vector.tensor_scalar(by_runs_out(grouped), by_runs_in(picked[h][:]), -1.0, None, ALU.mult)
+                else:
+                    nc.scalar.activation(by_runs_out(grouped), by_runs_in(picked[h][:]), ACT.Copy, scale=-1.0)
+                x_q[a, h] = quantize(grouped, f"x_{a}{h}")
+                first_product(a, 0, h)
+
+        h_q = {}
+        for b in range(PASSES_2):
+            if b == 1:
+                for h in range(HALVES):
+                    for a in range(PASSES_1):
+                        first_product(a, b, h)
+            sig = [ring.tile([P, 2, HALVES, COLS], F32, name="sig", tag="big", bufs=10) for u in range(2)]
+            log = [ring.tile([P, 2, HALVES, COLS], F32, name="log", tag="big", bufs=10) for u in range(2)]
+            low = [ring.tile([P, PACK, COLS], F32, name="low", tag="big", bufs=10) for h in range(HALVES)]
+            for h in range(HALVES):
+                for t in range(PACK):
+                    nc.scalar.activation(sig[t // 2][:, t % 2, h, :], banks[h, t][:], ACT.Sigmoid, bias=neg_bias[:, b, t : t + 1])
+            if b == 0:
+                for a in range(PASSES_1):
+                    w1_q[a, 1] = quantize(group_w1(a, 1, False), f"w1_{a}1")
+            for t in range(PACK):
+                nc.scalar.activation(log[t // 2][:, t % 2, :, :], sig[t // 2][:, t % 2, :, :], ACT.Ln, bias=TINY)
+                for h in range(HALVES):
+                    nc.vector.scalar_tensor_tensor(
+                        low[h][:, t, :], banks[h, t][:], neg_bias[:, b, t : t + 1], log[t // 2][:, t % 2, h, :], ALU.add, ALU.min
+                    )
+            for h in range(HALVES):
+                last = (b, h) == (PASSES_2 - 1, HALVES - 1)
+                cols = P if last else COLS
+                for c in range(COLS // cols):
+                    grouped = ring.tile([P, PACK * cols], BF16, name="h_grouped", bufs=3, align_bytes=64)
+                    spread = neg_gains[:, b, :].unsqueeze(1).unsqueeze(3).to_broadcast([P, cols // RUN, PACK, RUN])
+                    nc.vector.tensor_tensor(by_runs_out(grouped), by_runs_in(low[h][:, :, c * cols : (c + 1) * cols]), spread, ALU.mult)
+                    h_q[b, h, c] = quantize(grouped, f"h_{b}{h}{c}", cols)
+
+        def second_product(acc, n, b, codes, scales):
+            nc.tensor.matmul_mx(
+                out=acc,
+                lhsT=w2_code[:, b, 2 * n * P : 2 * (n + 1) * P].bitcast(FP4X4),
+                lhsT_scale=w2_scale[:, b * N + n * P : b * N + (n + 1) * P],
+                rhs=codes.bitcast(FP8X4),
+                rhs_scale=scales,
+                start=(b == 0),
+                stop=(b == PASSES_2 - 1),
+            )
+
+        for n in range(N // P):
+            acc = psum.tile([P, COLS], F32, name=f"bank0{n}")
+            for b in range(PASSES_2):
+                h_codes, h_scales = h_q[b, 0, 0]
+                second_product(acc[:], n, b, h_codes[:], h_scales[:])
+            result = ring.tile([P, COLS], F32, name="result", bufs=8)
+            nc.scalar.copy(result[:], acc[:])
+            nc.sync.dma_start(out[n * P : (n + 1) * P, 0:COLS], result[:])
+        for c in range(COLS // P):
+            acc = psum.tile([P, COLS], F32, name=f"bank1{c}")
+            for n in range(N // P):
+                h_codes, h_scales = h_q[0, 1, 0]
+                second_product(acc[:, n * P : (n + 1) * P], n, 0, h_codes[:, c * P : (c + 1) * P], h_scales[:, c * P : (c + 1) * P])
+                h_codes, h_scales = h_q[1, 1, c]
+                second_product(acc[:, n * P : (n + 1) * P], n, 1, h_codes[:], h_scales[:])
+            result = ring.tile([P, COLS], F32, name="result", bufs=8)
+            nc.scalar.copy(result[:], acc[:])
+            nc.sync.dma_start(
+                out[:, COLS + c * P : COLS + (c + 1) * P].rearrange("(n p) c -> p n c", p=P),
+                result[:].rearrange("p (n c) -> p n c", c=P),
+            )

@@ -25,6 +25,9 @@ PASSES_1 = K // K_PASS
 PASSES_2 = H // K_PASS
 HALVES = S // COLS
 TINY = 2.0**-60
+W1_AFTER = {(1, 0): 0, (1, 2): 1, (2, 1): 2}
+CODES_IN_SLOT = {"x_00": 4, "x_01": 5, "w1_00": 6, "w1_10": 7, "x_10": 8, "x_11": 9}
+EPILOGUE_SLOTS = [[0, 1, 2, 3], [6, 7, 10, 11]]
 
 
 def tile_list_book_intensity_risk_kernel(tc, xT, wgt, offs, w1, b1, gain, w2_words, w2_scales, out):
@@ -41,42 +44,45 @@ def tile_list_book_intensity_risk_kernel(tc, xT, wgt, offs, w1, b1, gain, w2_wor
         nc.gpsimd.memset(warm[:, 0:1], 0.0)
         nc.scalar.activation(warm[:, 1:2], warm[:, 0:1], ACT.Sigmoid)
 
-        bias = keep.tile([P, PASSES_2, PACK], F32, name="bias")
-        nc.gpsimd.dma_start(bias[:], b1.rearrange("(b p t) -> p b t", p=P, t=PACK))
-        gains = keep.tile([P, PASSES_2, PACK], F32, name="gains")
-        nc.gpsimd.dma_start(gains[:], gain.rearrange("(b p t) -> p b t", p=P, t=PACK))
-        neg_bias = keep.tile([P, PASSES_2, PACK], F32, name="neg_bias")
-        nc.gpsimd.tensor_scalar(neg_bias[:], bias[:], -1.0, 0.0, ALU.mult, ALU.add)
-        neg_gains = keep.tile([P, PASSES_2, PACK], F32, name="neg_gains")
-        nc.gpsimd.tensor_scalar(neg_gains[:], gains[:], -1.0, 0.0, ALU.mult, ALU.add)
         w2_scale = keep.tile([P, PASSES_2 * N], U8, name="w2_scale", align_bytes=64)
         nc.gpsimd.memset(w2_scale[:].bitcast(I32), 0)
 
-        weights = [keep.tile([P, COLS], F32, name=f"weights{h}") for h in range(HALVES)]
+        picked_last = keep.tile([P, PACK, COLS], F32, name="picked_last")
+        weights_1 = keep.tile([P, COLS], F32, name="weights_1")
+        weights = [picked_last[:, PACK - 2, :], weights_1[:]]
         planes = {}
         w1_raw = {}
 
         def load_plane(a, i):
-            planes[a, i] = ring.tile([P, T], F32, name="plane", tag="big", bufs=10)
+            planes[a, i] = ring.tile([P, T], F32, name="plane", tag=f"slot{PACK * a + i}", bufs=1, align_bytes=64)
             rows = xT[a * K_PASS : (a + 1) * K_PASS, :].rearrange("(p i) t -> p i t", i=PACK)
             nc.sync.dma_start(planes[a, i][:], rows[:, i, :])
 
         def load_w1(a, b):
-            w1_raw[a, b] = ring.tile([P, PACK, K_PASS], F32, name="w1_raw", bufs=3)
+            if (a, b) == (0, 1):
+                w1_raw[a, b] = ring.tile([P, PACK, K_PASS], F32, name="w1_raw01", tag="raw01", bufs=1, align_bytes=64)
+            else:
+                w1_raw[a, b] = ring.tile([P, PACK, K_PASS], F32, name="w1_raw", bufs=2)
             rows = w1[a * K_PASS : (a + 1) * K_PASS, b * K_PASS : (b + 1) * K_PASS]
             nc.sync.dma_start(w1_raw[a, b][:], rows.rearrange("(p i) r -> p i r", i=PACK))
 
-        nc.sync.dma_start(weights[0][:], wgt[:, 0:COLS])
+        nc.sync.dma_start(weights[0], wgt[:, 0:COLS])
         load_plane(0, 0)
-        nc.sync.dma_start(weights[1][:], wgt[:, COLS:S])
+        nc.sync.dma_start(weights[1], wgt[:, COLS:S])
         for a in range(PASSES_1):
             for i in range(PACK):
                 if (a, i) != (0, 0):
                     load_plane(a, i)
-                if i == 1:
-                    load_w1(a, 0)
+                if (a, i) in W1_AFTER:
+                    load_w1(W1_AFTER[a, i], 0)
+        bias = keep.tile([P, PASSES_2, PACK], F32, name="bias")
+        nc.sync.dma_start(bias[:], b1.rearrange("(b p t) -> p b t", p=P, t=PACK))
+        neg_bias = keep.tile([P, PASSES_2, PACK], F32, name="neg_bias")
+        nc.gpsimd.tensor_scalar(neg_bias[:], bias[:], -1.0, 0.0, ALU.mult, ALU.add)
         for a in range(PASSES_1):
             load_w1(a, 1)
+        gains = keep.tile([P, PASSES_2, PACK], F32, name="gains")
+        nc.sync.dma_start(gains[:], gain.rearrange("(b p t) -> p b t", p=P, t=PACK))
 
         w2_code = keep.tile([P, PASSES_2, 2 * N], U8, name="w2_code", align_bytes=64)
         nc.sync.dma_start(w2_code[:].bitcast(I32), w2_words.rearrange("b p c -> p b c").bitcast(I32))
@@ -87,36 +93,39 @@ def tile_list_book_intensity_risk_kernel(tc, xT, wgt, offs, w1, b1, gain, w2_wor
             )
 
         def quantize(grouped, name, cols=COLS):
-            codes = keep.tile([P, cols], U32, name=name + "_codes", align_bytes=64)
+            if name in CODES_IN_SLOT:
+                codes = ring.tile([P, cols], U32, name=name + "_codes", tag=f"slot{CODES_IN_SLOT[name]}", bufs=1, align_bytes=64)
+            else:
+                codes = keep.tile([P, cols], U32, name=name + "_codes", align_bytes=64)
             scales = keep.tile([P, cols], U8, name=name + "_scales", align_bytes=64)
             nc.vector.quantize_mx(out=codes[:].bitcast(FP8X4), scales=scales[:], in_=grouped[:])
             return codes, scales
 
-        def by_runs_out(grouped):
-            return grouped[:].rearrange("p (c i t) -> p c t i", i=RUN, t=PACK)
+        def by_runs_out(grouped, run=RUN):
+            return grouped[:].rearrange("p (c i t) -> p c t i", i=run, t=PACK)
 
-        def by_runs_in(four):
-            return four.rearrange("p t (c i) -> p c t i", i=RUN)
+        def by_runs_in(four, run=RUN):
+            return four.rearrange("p t (c i) -> p c t i", i=run)
 
         def group_w1(a, b, on_scalar):
             if on_scalar:
                 grouped = ring.tile([P, PACK * K_PASS], BF16, name="w1_grouped", bufs=1, align_bytes=64)
             else:
-                grouped = ring.tile([P, PACK * K_PASS], BF16, name="w1_late", tag=f"late{a % 2}", bufs=1, align_bytes=64)
+                grouped = ring.tile([P, PACK * K_PASS], BF16, name="w1_late", tag=["late0", "raw01", "late1"][a], bufs=1, align_bytes=64)
             dst = grouped[:].rearrange("p (t m i) -> p m i t", t=PACK, i=PACK)
             src = w1_raw[a, b][:].rearrange("p i (m t) -> p m i t", t=PACK)
             if on_scalar:
                 nc.scalar.copy(dst, src)
             else:
-                nc.vector.tensor_copy(dst, src)
+                nc.vector.tensor_copy(dst.rearrange("p m i t -> p m t i"), src.rearrange("p m i t -> p m t i"))
             return grouped
 
         w1_q = {}
         x_q = {}
         banks = {}
 
-        def first_product(a, b, h):
-            for t in range(PACK):
+        def first_product(a, b, h, slots=range(PACK)):
+            for t in slots:
                 if a == 0:
                     banks[h, t] = psum.tile([P, COLS], F32, name=f"bank{h}{t}")
                 w_codes, w_scales = w1_q[a, b]
@@ -132,82 +141,135 @@ def tile_list_book_intensity_risk_kernel(tc, xT, wgt, offs, w1, b1, gain, w2_wor
                 )
 
         for a in range(PASSES_1):
-            picked = [ring.tile([P, PACK, COLS], F32, name="picked", bufs=4) for h in range(HALVES)]
+            picked = [
+                picked_last if (a, h) == (PASSES_1 - 1, HALVES - 1) else ring.tile([P, PACK, COLS], F32, name="picked", bufs=3)
+                for h in range(HALVES)
+            ]
             for i in range(PACK):
                 for h in range(HALVES):
                     lists = offsets[:, h * COLS // 16 : (h + 1) * COLS // 16]
-                    nc.vector.tensor_tensor(picked[h][:, i, :], planes[a, i][:].indirect(lists), weights[h][:], ALU.mult)
-                if i == 1:
-                    w_grouped = group_w1(a, 0, True)
-                if i == 2:
-                    w1_q[a, 0] = quantize(w_grouped, f"w1_{a}0")
+                    if (a, i, h) == (PASSES_1 - 1, PACK - 2, 1):
+                        continue
+                    if (a, i, h) == (PASSES_1 - 1, PACK - 1, 1):
+                        nc.vector.tensor_tensor(picked[h][:, i - 1, :], planes[a, i - 1][:].indirect(lists), weights[h], ALU.mult)
+                    nc.vector.tensor_tensor(picked[h][:, i, :], planes[a, i][:].indirect(lists), weights[h], ALU.mult)
+            if a == PASSES_1 - 1:
+                w1_q[a, 0] = quantize(group_w1(a, 0, True), f"w1_{a}0")
+            x_grouped = []
             for h in range(HALVES):
-                grouped = ring.tile([P, PACK * COLS], BF16, name="x_grouped", tag=f"late{h}", bufs=1, align_bytes=64)
                 if (a, h) == (PASSES_1 - 1, HALVES - 1):
+                    grouped = ring.tile([P, PACK * COLS], BF16, name="x_grouped", tag="late0", bufs=1, align_bytes=64)
                     nc.vector.tensor_scalar(by_runs_out(grouped), by_runs_in(picked[h][:]), -1.0, None, ALU.mult)
                 else:
+                    grouped = ring.tile([P, PACK * COLS], BF16, name="x_grouped", tag=f"late{h}", bufs=1, align_bytes=64)
                     nc.scalar.activation(by_runs_out(grouped), by_runs_in(picked[h][:]), ACT.Copy, scale=-1.0)
                 x_q[a, h] = quantize(grouped, f"x_{a}{h}")
+            if a < PASSES_1 - 1:
+                w1_q[a, 0] = quantize(group_w1(a, 0, True), f"w1_{a}0")
+            for h in range(HALVES):
                 first_product(a, 0, h)
 
         h_q = {}
         for b in range(PASSES_2):
             if b == 1:
                 for h in range(HALVES):
-                    for a in range(PASSES_1):
-                        first_product(a, b, h)
-            sig = [ring.tile([P, 2, HALVES, COLS], F32, name="sig", tag="big", bufs=10) for u in range(2)]
-            log = [ring.tile([P, 2, HALVES, COLS], F32, name="log", tag="big", bufs=10) for u in range(2)]
-            low = [ring.tile([P, PACK, COLS], F32, name="low", tag="big", bufs=10) for h in range(HALVES)]
+                    for t in range(PACK):
+                        for a in range(PASSES_1):
+                            first_product(a, b, h, [t])
+            sig = [ring.tile([P, PACK, COLS], F32, name="sig", tag=f"slot{EPILOGUE_SLOTS[b][h]}", bufs=1, align_bytes=64) for h in range(HALVES)]
+            log = [ring.tile([P, PACK, COLS], F32, name="log", tag=f"slot{EPILOGUE_SLOTS[b][HALVES + h]}", bufs=1, align_bytes=64) for h in range(HALVES)]
+            low = sig
             for h in range(HALVES):
                 for t in range(PACK):
-                    nc.scalar.activation(sig[t // 2][:, t % 2, h, :], banks[h, t][:], ACT.Sigmoid, bias=neg_bias[:, b, t : t + 1])
+                    nc.scalar.activation(sig[h][:, t, :], banks[h, t][:], ACT.Sigmoid, bias=neg_bias[:, b, t : t + 1])
             if b == 0:
                 for a in range(PASSES_1):
                     w1_q[a, 1] = quantize(group_w1(a, 1, False), f"w1_{a}1")
-            for t in range(PACK):
-                nc.scalar.activation(log[t // 2][:, t % 2, :, :], sig[t // 2][:, t % 2, :, :], ACT.Ln, bias=TINY)
-                for h in range(HALVES):
-                    nc.vector.scalar_tensor_tensor(
-                        low[h][:, t, :], banks[h, t][:], neg_bias[:, b, t : t + 1], log[t // 2][:, t % 2, h, :], ALU.add, ALU.min
+            if b == 1:
+                scaled = ring.tile([P, PACK, COLS], F32, name="scaled", tag="slot2", bufs=1, align_bytes=64)
+                for t in range(PACK):
+                    nc.vector.tensor_scalar(
+                        scaled[:, t, :], banks[0, t][:], neg_bias[:, b, t : t + 1], gains[:, b, t : t + 1], ALU.add, ALU.mult
                     )
-            for h in range(HALVES):
+            tiny = keep.tile([P, 1], F32, name=f"tiny{b}")
+            nc.scalar.activation(tiny[:], sig[HALVES - 1][:, PACK - 1, 0:1], ACT.Identity, scale=0.0, bias=TINY)
+
+            def logs(h):
+                for t in range(PACK):
+                    nc.scalar.activation(log[h][:, t, :], sig[h][:, t, :], ACT.Ln, bias=tiny[:])
+                    if (b, h) == (1, 0):
+                        nc.vector.scalar_tensor_tensor(
+                            low[h][:, t, :], log[h][:, t, :], gains[:, b, t : t + 1], scaled[:, t, :], ALU.mult, ALU.min
+                        )
+                    else:
+                        nc.vector.scalar_tensor_tensor(
+                            low[h][:, t, :], banks[h, t][:], neg_bias[:, b, t : t + 1], log[h][:, t, :], ALU.add, ALU.min
+                        )
+
+            def intensities(h):
                 last = (b, h) == (PASSES_2 - 1, HALVES - 1)
                 cols = P if last else COLS
                 for c in range(COLS // cols):
                     grouped = ring.tile([P, PACK * cols], BF16, name="h_grouped", bufs=3, align_bytes=64)
-                    spread = neg_gains[:, b, :].unsqueeze(1).unsqueeze(3).to_broadcast([P, cols // RUN, PACK, RUN])
-                    nc.vector.tensor_tensor(by_runs_out(grouped), by_runs_in(low[h][:, :, c * cols : (c + 1) * cols]), spread, ALU.mult)
+                    spread = gains[:, b, :].unsqueeze(1).unsqueeze(3).to_broadcast([P, cols // 2, PACK, 2])
+                    if (b, h) == (1, 0):
+                        nc.vector.tensor_copy(by_runs_out(grouped), by_runs_in(low[h][:]))
+                    else:
+                        nc.vector.tensor_tensor(by_runs_out(grouped, 2), by_runs_in(low[h][:, :, c * cols : (c + 1) * cols], 2), spread, ALU.mult)
                     h_q[b, h, c] = quantize(grouped, f"h_{b}{h}{c}", cols)
 
-        def second_product(acc, n, b, codes, scales):
+            if b == 0:
+                logs(0)
+                logs(1)
+                intensities(0)
+                intensities(1)
+            else:
+                logs(0)
+                intensities(0)
+                logs(1)
+                intensities(1)
+
+        def second_product(acc, n, b, codes, scales, start, stop):
             nc.tensor.matmul_mx(
                 out=acc,
                 lhsT=w2_code[:, b, 2 * n * P : 2 * (n + 1) * P].bitcast(FP4X4),
                 lhsT_scale=w2_scale[:, b * N + n * P : b * N + (n + 1) * P],
                 rhs=codes.bitcast(FP8X4),
                 rhs_scale=scales,
-                start=(b == 0),
-                stop=(b == PASSES_2 - 1),
+                start=start,
+                stop=stop,
             )
 
         for n in range(N // P):
             acc = psum.tile([P, COLS], F32, name=f"bank0{n}")
             for b in range(PASSES_2):
                 h_codes, h_scales = h_q[b, 0, 0]
-                second_product(acc[:], n, b, h_codes[:], h_scales[:])
+                second_product(acc[:], n, b, h_codes[:], h_scales[:], b == 0, b == 1)
             result = ring.tile([P, COLS], F32, name="result", bufs=8)
-            nc.scalar.copy(result[:], acc[:])
+            nc.scalar.mul(result[:], acc[:], -1.0)
             nc.sync.dma_start(out[n * P : (n + 1) * P, 0:COLS], result[:])
         for c in range(COLS // P):
-            acc = psum.tile([P, COLS], F32, name=f"bank1{c}")
-            for n in range(N // P):
-                h_codes, h_scales = h_q[0, 1, 0]
-                second_product(acc[:, n * P : (n + 1) * P], n, 0, h_codes[:, c * P : (c + 1) * P], h_scales[:, c * P : (c + 1) * P])
-                h_codes, h_scales = h_q[1, 1, c]
-                second_product(acc[:, n * P : (n + 1) * P], n, 1, h_codes[:], h_scales[:])
+            last = c == COLS // P - 1
+            early = [tile[:, c * P : (c + 1) * P] for tile in h_q[0, 1, 0]]
+            late = [tile[:] for tile in h_q[1, 1, c]]
             result = ring.tile([P, COLS], F32, name="result", bufs=8)
-            nc.scalar.copy(result[:], acc[:])
+            if last:
+                accs = [psum.tile([P, P], F32, name=f"bank0{n}") for n in range(N // P)]
+                for n in range(N // P):
+                    second_product(accs[n][:], n, 0, *early, True, False)
+                for n in range(N // P):
+                    second_product(accs[n][:], n, 1, *late, False, True)
+                    if n % 2 == 0:
+                        nc.scalar.mul(result[:, n * P : (n + 1) * P], accs[n][:], -1.0)
+                    else:
+                        nc.vector.tensor_scalar(result[:, n * P : (n + 1) * P], accs[n][:], -1.0, None, ALU.mult)
+            else:
+                acc = psum.tile([P, COLS], F32, name=f"bank1{c}")
+                for n in range(N // P):
+                    second_product(acc[:, n * P : (n + 1) * P], n, 0, *early, n == 0, False)
+                for n in range(N // P):
+                    second_product(acc[:, n * P : (n + 1) * P], n, 1, *late, False, n == N // P - 1)
+                nc.scalar.mul(result[:], acc[:], -1.0)
             nc.sync.dma_start(
                 out[:, COLS + c * P : COLS + (c + 1) * P].rearrange("(n p) c -> p n c", p=P),
                 result[:].rearrange("p (n c) -> p n c", c=P),

@@ -27,7 +27,6 @@ HALVES = S // COLS
 TINY = 2.0**-60
 W1_AFTER = {(1, 0): 0, (1, 2): 1, (2, 1): 2}
 CODES_IN_SLOT = {"x_00": 4, "x_01": 5, "w1_00": 6, "w1_10": 7, "x_10": 8, "x_11": 9}
-EPILOGUE_SLOTS = [[0, 1, 2, 3], [6, 7, 10, 11]]
 
 
 def tile_list_book_intensity_risk_kernel(tc, xT, wgt, offs, w1, b1, gain, w2_words, w2_scales, out):
@@ -47,38 +46,38 @@ def tile_list_book_intensity_risk_kernel(tc, xT, wgt, offs, w1, b1, gain, w2_wor
         w2_scale = keep.tile([P, PASSES_2 * N], U8, name="w2_scale", align_bytes=64)
         nc.gpsimd.memset(w2_scale[:].bitcast(I32), 0)
 
-        picked_last = keep.tile([P, PACK, COLS], F32, name="picked_last")
-        weights_1 = keep.tile([P, COLS], F32, name="weights_1")
+        picked_last = keep.tile([P, PACK, COLS], F32, name="picked_last", align_bytes=256)
+        weights_1 = keep.tile([P, COLS], F32, name="weights_1", align_bytes=256)
         weights = [picked_last[:, PACK - 2, :], weights_1[:]]
         planes = {}
         w1_raw = {}
 
         def load_plane(a, i):
-            planes[a, i] = ring.tile([P, T], F32, name="plane", tag=f"slot{PACK * a + i}", bufs=1, align_bytes=64)
+            planes[a, i] = ring.tile([P, T], F32, name="plane", tag=f"slot{PACK * a + i}", bufs=1, align_bytes=256)
             rows = xT[a * K_PASS : (a + 1) * K_PASS, :].rearrange("(p i) t -> p i t", i=PACK)
             nc.sync.dma_start(planes[a, i][:], rows[:, i, :])
 
         def load_w1(a, b):
             if (a, b) == (0, 1):
-                w1_raw[a, b] = ring.tile([P, PACK, K_PASS], F32, name="w1_raw01", tag="raw01", bufs=1, align_bytes=64)
+                w1_raw[a, b] = ring.tile([P, PACK, K_PASS], F32, name="w1_raw01", tag="raw01", bufs=1, align_bytes=256)
             else:
-                w1_raw[a, b] = ring.tile([P, PACK, K_PASS], F32, name="w1_raw", bufs=2)
+                w1_raw[a, b] = ring.tile([P, PACK, K_PASS], F32, name="w1_raw", bufs=2, align_bytes=256)
             rows = w1[a * K_PASS : (a + 1) * K_PASS, b * K_PASS : (b + 1) * K_PASS]
             nc.sync.dma_start(w1_raw[a, b][:], rows.rearrange("(p i) r -> p i r", i=PACK))
 
         nc.sync.dma_start(weights[0], wgt[:, 0:COLS])
         load_plane(0, 0)
         nc.sync.dma_start(weights[1], wgt[:, COLS:S])
+        bias = keep.tile([P, PASSES_2, PACK], F32, name="bias")
+        nc.sync.dma_start(bias[:], b1.rearrange("(b p t) -> p b t", p=P, t=PACK))
+        neg_bias = keep.tile([P, PASSES_2, PACK], F32, name="neg_bias")
+        nc.gpsimd.tensor_scalar(neg_bias[:], bias[:], -1.0, 0.0, ALU.mult, ALU.add)
         for a in range(PASSES_1):
             for i in range(PACK):
                 if (a, i) != (0, 0):
                     load_plane(a, i)
                 if (a, i) in W1_AFTER:
                     load_w1(W1_AFTER[a, i], 0)
-        bias = keep.tile([P, PASSES_2, PACK], F32, name="bias")
-        nc.sync.dma_start(bias[:], b1.rearrange("(b p t) -> p b t", p=P, t=PACK))
-        neg_bias = keep.tile([P, PASSES_2, PACK], F32, name="neg_bias")
-        nc.gpsimd.tensor_scalar(neg_bias[:], bias[:], -1.0, 0.0, ALU.mult, ALU.add)
         for a in range(PASSES_1):
             load_w1(a, 1)
         gains = keep.tile([P, PASSES_2, PACK], F32, name="gains")
@@ -94,7 +93,7 @@ def tile_list_book_intensity_risk_kernel(tc, xT, wgt, offs, w1, b1, gain, w2_wor
 
         def quantize(grouped, name, cols=COLS):
             if name in CODES_IN_SLOT:
-                codes = ring.tile([P, cols], U32, name=name + "_codes", tag=f"slot{CODES_IN_SLOT[name]}", bufs=1, align_bytes=64)
+                codes = ring.tile([P, cols], U32, name=name + "_codes", tag=f"slot{CODES_IN_SLOT[name]}", bufs=1, align_bytes=256)
             else:
                 codes = keep.tile([P, cols], U32, name=name + "_codes", align_bytes=64)
             scales = keep.tile([P, cols], U8, name=name + "_scales", align_bytes=64)
@@ -111,7 +110,7 @@ def tile_list_book_intensity_risk_kernel(tc, xT, wgt, offs, w1, b1, gain, w2_wor
             if on_scalar:
                 grouped = ring.tile([P, PACK * K_PASS], BF16, name="w1_grouped", bufs=1, align_bytes=64)
             else:
-                grouped = ring.tile([P, PACK * K_PASS], BF16, name="w1_late", tag=["late0", "raw01", "late1"][a], bufs=1, align_bytes=64)
+                grouped = ring.tile([P, PACK * K_PASS], BF16, name="w1_late", tag=["late0", "raw01", "late1"][a], bufs=1, align_bytes=256)
             dst = grouped[:].rearrange("p (t m i) -> p m i t", t=PACK, i=PACK)
             src = w1_raw[a, b][:].rearrange("p i (m t) -> p m i t", t=PACK)
             if on_scalar:
@@ -158,10 +157,10 @@ def tile_list_book_intensity_risk_kernel(tc, xT, wgt, offs, w1, b1, gain, w2_wor
             x_grouped = []
             for h in range(HALVES):
                 if (a, h) == (PASSES_1 - 1, HALVES - 1):
-                    grouped = ring.tile([P, PACK * COLS], BF16, name="x_grouped", tag="late0", bufs=1, align_bytes=64)
+                    grouped = ring.tile([P, PACK * COLS], BF16, name="x_grouped", tag="late0", bufs=1, align_bytes=256)
                     nc.vector.tensor_scalar(by_runs_out(grouped), by_runs_in(picked[h][:]), -1.0, None, ALU.mult)
                 else:
-                    grouped = ring.tile([P, PACK * COLS], BF16, name="x_grouped", tag=f"late{h}", bufs=1, align_bytes=64)
+                    grouped = ring.tile([P, PACK * COLS], BF16, name="x_grouped", tag=f"late{h}", bufs=1, align_bytes=256)
                     nc.scalar.activation(by_runs_out(grouped), by_runs_in(picked[h][:]), ACT.Copy, scale=-1.0)
                 x_q[a, h] = quantize(grouped, f"x_{a}{h}")
             if a < PASSES_1 - 1:
@@ -170,64 +169,58 @@ def tile_list_book_intensity_risk_kernel(tc, xT, wgt, offs, w1, b1, gain, w2_wor
                 first_product(a, 0, h)
 
         h_q = {}
-        for b in range(PASSES_2):
-            if b == 1:
-                for h in range(HALVES):
-                    for t in range(PACK):
-                        for a in range(PASSES_1):
-                            first_product(a, b, h, [t])
-            sig = [ring.tile([P, PACK, COLS], F32, name="sig", tag=f"slot{EPILOGUE_SLOTS[b][h]}", bufs=1, align_bytes=64) for h in range(HALVES)]
-            log = [ring.tile([P, PACK, COLS], F32, name="log", tag=f"slot{EPILOGUE_SLOTS[b][HALVES + h]}", bufs=1, align_bytes=64) for h in range(HALVES)]
-            low = sig
+
+        def slot_tile(shape, name, slot):
+            return ring.tile(shape, F32, name=name, tag=f"slot{slot}", bufs=1, align_bytes=256)
+
+        def with_gain(low, b, h, cols):
+            for c in range(COLS // cols):
+                grouped = ring.tile([P, PACK * cols], BF16, name="h_grouped", bufs=3, align_bytes=64)
+                spread = gains[:, b, :].unsqueeze(1).unsqueeze(3).to_broadcast([P, cols // 2, PACK, 2])
+                nc.vector.tensor_tensor(by_runs_out(grouped, 2), by_runs_in(low[:, :, c * cols : (c + 1) * cols], 2), spread, ALU.mult)
+                h_q[b, h, c] = quantize(grouped, f"h_{b}{h}{c}", cols)
+
+        sig = [slot_tile([P, 2, HALVES, COLS], "sig", u) for u in range(2)]
+        log = [slot_tile([P, 2, HALVES, COLS], "log", 2 + u) for u in range(2)]
+        low = [slot_tile([P, PACK, COLS], "low", 6 + h) for h in range(HALVES)]
+        for h in range(HALVES):
+            for t in range(PACK):
+                nc.scalar.activation(sig[t // 2][:, t % 2, h, :], banks[h, t][:], ACT.Sigmoid, bias=neg_bias[:, 0, t : t + 1])
+        for a in range(PASSES_1):
+            w1_q[a, 1] = quantize(group_w1(a, 1, False), f"w1_{a}1")
+        for t in range(PACK):
+            nc.scalar.activation(log[t // 2][:, t % 2], sig[t // 2][:, t % 2], ACT.Ln, bias=TINY)
             for h in range(HALVES):
-                for t in range(PACK):
-                    nc.scalar.activation(sig[h][:, t, :], banks[h, t][:], ACT.Sigmoid, bias=neg_bias[:, b, t : t + 1])
-            if b == 0:
+                nc.vector.scalar_tensor_tensor(
+                    low[h][:, t, :], banks[h, t][:], neg_bias[:, 0, t : t + 1], log[t // 2][:, t % 2, h, :], ALU.add, ALU.min
+                )
+        for h in range(HALVES):
+            with_gain(low[h], 0, h, COLS)
+
+        for h in range(HALVES):
+            for t in range(PACK):
                 for a in range(PASSES_1):
-                    w1_q[a, 1] = quantize(group_w1(a, 1, False), f"w1_{a}1")
-            if b == 1:
-                scaled = ring.tile([P, PACK, COLS], F32, name="scaled", tag="slot2", bufs=1, align_bytes=64)
-                for t in range(PACK):
-                    nc.vector.tensor_scalar(
-                        scaled[:, t, :], banks[0, t][:], neg_bias[:, b, t : t + 1], gains[:, b, t : t + 1], ALU.add, ALU.mult
-                    )
-            tiny = keep.tile([P, 1], F32, name=f"tiny{b}")
-            nc.scalar.activation(tiny[:], sig[HALVES - 1][:, PACK - 1, 0:1], ACT.Identity, scale=0.0, bias=TINY)
-
-            def logs(h):
-                for t in range(PACK):
-                    nc.scalar.activation(log[h][:, t, :], sig[h][:, t, :], ACT.Ln, bias=tiny[:])
-                    if (b, h) == (1, 0):
-                        nc.vector.scalar_tensor_tensor(
-                            low[h][:, t, :], log[h][:, t, :], gains[:, b, t : t + 1], scaled[:, t, :], ALU.mult, ALU.min
-                        )
-                    else:
-                        nc.vector.scalar_tensor_tensor(
-                            low[h][:, t, :], banks[h, t][:], neg_bias[:, b, t : t + 1], log[h][:, t, :], ALU.add, ALU.min
-                        )
-
-            def intensities(h):
-                last = (b, h) == (PASSES_2 - 1, HALVES - 1)
-                cols = P if last else COLS
-                for c in range(COLS // cols):
-                    grouped = ring.tile([P, PACK * cols], BF16, name="h_grouped", bufs=3, align_bytes=64)
-                    spread = gains[:, b, :].unsqueeze(1).unsqueeze(3).to_broadcast([P, cols // 2, PACK, 2])
-                    if (b, h) == (1, 0):
-                        nc.vector.tensor_copy(by_runs_out(grouped), by_runs_in(low[h][:]))
-                    else:
-                        nc.vector.tensor_tensor(by_runs_out(grouped, 2), by_runs_in(low[h][:, :, c * cols : (c + 1) * cols], 2), spread, ALU.mult)
-                    h_q[b, h, c] = quantize(grouped, f"h_{b}{h}{c}", cols)
-
-            if b == 0:
-                logs(0)
-                logs(1)
-                intensities(0)
-                intensities(1)
-            else:
-                logs(0)
-                intensities(0)
-                logs(1)
-                intensities(1)
+                    first_product(a, 1, h, [t])
+        sig = [slot_tile([P, PACK, COLS], "sig", h) for h in range(HALVES)]
+        log = [slot_tile([P, PACK, COLS], "log", 2 + h) for h in range(HALVES)]
+        for h in range(HALVES):
+            for t in range(PACK):
+                nc.scalar.activation(sig[h][:, t, :], banks[h, t][:], ACT.Sigmoid, bias=neg_bias[:, 1, t : t + 1])
+        scaled = slot_tile([P, PACK, COLS], "scaled", 10)
+        for t in range(PACK):
+            nc.vector.tensor_scalar(scaled[:, t, :], banks[0, t][:], neg_bias[:, 1, t : t + 1], gains[:, 1, t : t + 1], ALU.add, ALU.mult)
+        tiny = keep.tile([P, 1], F32, name="tiny")
+        nc.scalar.activation(tiny[:], sig[1][:, PACK - 1, 0:1], ACT.Identity, scale=0.0, bias=TINY)
+        for t in range(PACK):
+            nc.scalar.activation(log[0][:, t, :], sig[0][:, t, :], ACT.Ln, bias=tiny[:])
+            nc.vector.scalar_tensor_tensor(sig[0][:, t, :], log[0][:, t, :], gains[:, 1, t : t + 1], scaled[:, t, :], ALU.mult, ALU.min)
+        grouped = ring.tile([P, PACK * COLS], BF16, name="h_grouped", bufs=3, align_bytes=64)
+        nc.vector.tensor_copy(by_runs_out(grouped), by_runs_in(sig[0][:]))
+        h_q[1, 0, 0] = quantize(grouped, "h_100")
+        for t in range(PACK):
+            nc.scalar.activation(log[1][:, t, :], sig[1][:, t, :], ACT.Ln, bias=tiny[:])
+            nc.vector.scalar_tensor_tensor(sig[1][:, t, :], banks[1, t][:], neg_bias[:, 1, t : t + 1], log[1][:, t, :], ALU.add, ALU.min)
+        with_gain(sig[1], 1, 1, P)
 
         def second_product(acc, n, b, codes, scales, start, stop):
             nc.tensor.matmul_mx(
@@ -245,14 +238,14 @@ def tile_list_book_intensity_risk_kernel(tc, xT, wgt, offs, w1, b1, gain, w2_wor
             for b in range(PASSES_2):
                 h_codes, h_scales = h_q[b, 0, 0]
                 second_product(acc[:], n, b, h_codes[:], h_scales[:], b == 0, b == 1)
-            result = ring.tile([P, COLS], F32, name="result", bufs=8)
+            result = ring.tile([P, COLS], F32, name="result", bufs=8, align_bytes=256)
             nc.scalar.mul(result[:], acc[:], -1.0)
             nc.sync.dma_start(out[n * P : (n + 1) * P, 0:COLS], result[:])
         for c in range(COLS // P):
             last = c == COLS // P - 1
             early = [tile[:, c * P : (c + 1) * P] for tile in h_q[0, 1, 0]]
             late = [tile[:] for tile in h_q[1, 1, c]]
-            result = ring.tile([P, COLS], F32, name="result", bufs=8)
+            result = ring.tile([P, COLS], F32, name="result", bufs=8, align_bytes=256)
             if last:
                 accs = [psum.tile([P, P], F32, name=f"bank0{n}") for n in range(N // P)]
                 for n in range(N // P):

from contextlib import ExitStack

import concourse.mybir as mybir

K, T, S, H, N = 1536, 2048, 1024, 1024, 512
FLOPS = 2 * K * H * S + 2 * H * N * S

F32 = mybir.dt.float32
BF16 = mybir.dt.bfloat16
I32 = mybir.dt.int32
U32 = mybir.dt.uint32
U16 = mybir.dt.uint16
U8 = mybir.dt.uint8
FP8X4 = mybir.dt.float8_e4m3fn_x4
FP4X4 = mybir.dt.float4_e2m1fn_x4
ALU = mybir.AluOpType
ACT = mybir.ActivationFunctionType

P = 128
PACK = 4
K_PASS = P * PACK
COLS = 512
RUN = 4
PASSES_1 = K // K_PASS
PASSES_2 = H // K_PASS
HALVES = S // COLS
TINY = 2.0**-60
W1_AFTER = {(1, 0): 0, (1, 2): 1, (2, 1): 2}
CODES_IN_SLOT = {"x_00": 4, "x_01": 5, "w1_00": 6, "w1_10": 7, "x_10": 8, "x_11": 9}


def tile_list_book_intensity_risk_kernel(tc, xT, wgt, offs, w1, b1, gain, w2_words, w2_scales, out):
    nc = tc.nc
    with ExitStack() as ctx:
        keep = ctx.enter_context(tc.tile_pool(name="keep", bufs=1))
        ring = ctx.enter_context(tc.tile_pool(name="ring", bufs=2))
        psum = ctx.enter_context(tc.psum_pool(name="psum", bufs=1))

        offsets = keep.tile([P, S // 16], U16, name="offsets")
        nc.sync.dma_start(offsets[:], offs)

        warm = keep.tile([P, 2], F32, name="warm")
        nc.gpsimd.memset(warm[:, 0:1], 0.0)
        nc.scalar.activation(warm[:, 1:2], warm[:, 0:1], ACT.Sigmoid)

        w2_scale = keep.tile([P, PASSES_2 * N], U8, name="w2_scale", align_bytes=64)
        nc.gpsimd.memset(w2_scale[:].bitcast(I32), 0)

        picked_last = keep.tile([P, PACK, COLS], F32, name="picked_last", align_bytes=256)
        weights_1 = keep.tile([P, COLS], F32, name="weights_1", align_bytes=256)
        weights = [picked_last[:, PACK - 2, :], weights_1[:]]
        planes = {}
        w1_raw = {}

        def load_plane(a, i):
            planes[a, i] = ring.tile([P, T], F32, name="plane", tag=f"slot{PACK * a + i}", bufs=1, align_bytes=256)
            rows = xT[a * K_PASS : (a + 1) * K_PASS, :].rearrange("(p i) t -> p i t", i=PACK)
            nc.sync.dma_start(planes[a, i][:], rows[:, i, :])

        def load_w1(a, b):
            if (a, b) == (0, 1):
                w1_raw[a, b] = ring.tile([P, PACK, K_PASS], F32, name="w1_raw01", tag="raw01", bufs=1, align_bytes=256)
            else:
                w1_raw[a, b] = ring.tile([P, PACK, K_PASS], F32, name="w1_raw", bufs=2, align_bytes=256)
            rows = w1[a * K_PASS : (a + 1) * K_PASS, b * K_PASS : (b + 1) * K_PASS]
            nc.sync.dma_start(w1_raw[a, b][:], rows.rearrange("(p i) r -> p i r", i=PACK))

        nc.sync.dma_start(weights[0], wgt[:, 0:COLS])
        load_plane(0, 0)
        nc.sync.dma_start(weights[1], wgt[:, COLS:S])
        bias = keep.tile([P, PASSES_2, PACK], F32, name="bias")
        nc.sync.dma_start(bias[:], b1.rearrange("(b p t) -> p b t", p=P, t=PACK))
        neg_bias = keep.tile([P, PASSES_2, PACK], F32, name="neg_bias")
        nc.gpsimd.tensor_scalar(neg_bias[:], bias[:], -1.0, 0.0, ALU.mult, ALU.add)
        for a in range(PASSES_1):
            for i in range(PACK):
                if (a, i) != (0, 0):
                    load_plane(a, i)
                if (a, i) in W1_AFTER:
                    load_w1(W1_AFTER[a, i], 0)
        for a in range(PASSES_1):
            load_w1(a, 1)
        gains = keep.tile([P, PASSES_2, PACK], F32, name="gains")
        nc.sync.dma_start(gains[:], gain.rearrange("(b p t) -> p b t", p=P, t=PACK))

        w2_code = keep.tile([P, PASSES_2, 2 * N], U8, name="w2_code", align_bytes=64)
        nc.sync.dma_start(w2_code[:].bitcast(I32), w2_words.rearrange("b p c -> p b c").bitcast(I32))
        for q in range(4):
            nc.sync.dma_start(
                w2_scale[32 * q : 32 * q + 4, :].rearrange("p (b n) -> p b n", b=PASSES_2).bitcast(I32),
                w2_scales[:, 4 * q : 4 * q + 4, :].rearrange("b r n -> r b n").bitcast(I32),
            )

        def quantize(grouped, name, cols=COLS):
            if name in CODES_IN_SLOT:
                codes = ring.tile([P, cols], U32, name=name + "_codes", tag=f"slot{CODES_IN_SLOT[name]}", bufs=1, align_bytes=256)
            else:
                codes = keep.tile([P, cols], U32, name=name + "_codes", align_bytes=64)
            scales = keep.tile([P, cols], U8, name=name + "_scales", align_bytes=64)
            nc.vector.quantize_mx(out=codes[:].bitcast(FP8X4), scales=scales[:], in_=grouped[:])
            return codes, scales

        def by_runs_out(grouped, run=RUN):
            return grouped[:].rearrange("p (c i t) -> p c t i", i=run, t=PACK)

        def by_runs_in(four, run=RUN):
            return four.rearrange("p t (c i) -> p c t i", i=run)

        def group_w1(a, b, on_scalar):
            if on_scalar:
                grouped = ring.tile([P, PACK * K_PASS], BF16, name="w1_grouped", bufs=1, align_bytes=64)
            else:
                grouped = ring.tile([P, PACK * K_PASS], BF16, name="w1_late", tag=["late0", "raw01", "late1"][a], bufs=1, align_bytes=256)
            dst = grouped[:].rearrange("p (t m i) -> p m i t", t=PACK, i=PACK)
            src = w1_raw[a, b][:].rearrange("p i (m t) -> p m i t", t=PACK)
            if on_scalar:
                nc.scalar.copy(dst, src)
            else:
                nc.vector.tensor_copy(dst.rearrange("p m i t -> p m t i"), src.rearrange("p m i t -> p m t i"))
            return grouped

        w1_q = {}
        x_q = {}
        banks = {}

        def first_product(a, b, h, slots=range(PACK)):
            for t in slots:
                if a == 0:
                    banks[h, t] = psum.tile([P, COLS], F32, name=f"bank{h}{t}")
                w_codes, w_scales = w1_q[a, b]
                x_codes, x_scales = x_q[a, h]
                nc.tensor.matmul_mx(
                    out=banks[h, t][:],
                    lhsT=w_codes[:, t * P : (t + 1) * P].bitcast(FP8X4),
                    lhsT_scale=w_scales[:, t * P : (t + 1) * P],
                    rhs=x_codes[:].bitcast(FP8X4),
                    rhs_scale=x_scales[:],
                    start=(a == 0),
                    stop=(a == PASSES_1 - 1),
                )

        for a in range(PASSES_1):
            picked = [
                picked_last if (a, h) == (PASSES_1 - 1, HALVES - 1) else ring.tile([P, PACK, COLS], F32, name="picked", bufs=3)
                for h in range(HALVES)
            ]
            for i in range(PACK):
                for h in range(HALVES):
                    lists = offsets[:, h * COLS // 16 : (h + 1) * COLS // 16]
                    if (a, i, h) == (PASSES_1 - 1, PACK - 2, 1):
                        continue
                    if (a, i, h) == (PASSES_1 - 1, PACK - 1, 1):
                        nc.vector.tensor_tensor(picked[h][:, i - 1, :], planes[a, i - 1][:].indirect(lists), weights[h], ALU.mult)
                    nc.vector.tensor_tensor(picked[h][:, i, :], planes[a, i][:].indirect(lists), weights[h], ALU.mult)
            if a == PASSES_1 - 1:
                w1_q[a, 0] = quantize(group_w1(a, 0, True), f"w1_{a}0")
            x_grouped = []
            for h in range(HALVES):
                if (a, h) == (PASSES_1 - 1, HALVES - 1):
                    grouped = ring.tile([P, PACK * COLS], BF16, name="x_grouped", tag="late0", bufs=1, align_bytes=256)
                    nc.vector.tensor_scalar(by_runs_out(grouped), by_runs_in(picked[h][:]), -1.0, None, ALU.mult)
                else:
                    grouped = ring.tile([P, PACK * COLS], BF16, name="x_grouped", tag=f"late{h}", bufs=1, align_bytes=256)
                    nc.scalar.activation(by_runs_out(grouped), by_runs_in(picked[h][:]), ACT.Copy, scale=-1.0)
                x_q[a, h] = quantize(grouped, f"x_{a}{h}")
            if a < PASSES_1 - 1:
                w1_q[a, 0] = quantize(group_w1(a, 0, True), f"w1_{a}0")
            for h in range(HALVES):
                first_product(a, 0, h)

        h_q = {}

        def slot_tile(shape, name, slot):
            return ring.tile(shape, F32, name=name, tag=f"slot{slot}", bufs=1, align_bytes=256)

        def with_gain(low, b, h, cols):
            for c in range(COLS // cols):
                grouped = ring.tile([P, PACK * cols], BF16, name="h_grouped", bufs=3, align_bytes=64)
                spread = gains[:, b, :].unsqueeze(1).unsqueeze(3).to_broadcast([P, cols // 2, PACK, 2])
                nc.vector.tensor_tensor(by_runs_out(grouped, 2), by_runs_in(low[:, :, c * cols : (c + 1) * cols], 2), spread, ALU.mult)
                h_q[b, h, c] = quantize(grouped, f"h_{b}{h}{c}", cols)

        sig = [slot_tile([P, 2, HALVES, COLS], "sig", u) for u in range(2)]
        log = [slot_tile([P, 2, HALVES, COLS], "log", 2 + u) for u in range(2)]
        low = [slot_tile([P, PACK, COLS], "low", 6 + h) for h in range(HALVES)]
        for h in range(HALVES):
            for t in range(PACK):
                nc.scalar.activation(sig[t // 2][:, t % 2, h, :], banks[h, t][:], ACT.Sigmoid, bias=neg_bias[:, 0, t : t + 1])
        for a in range(PASSES_1):
            w1_q[a, 1] = quantize(group_w1(a, 1, False), f"w1_{a}1")
        for t in range(PACK):
            nc.scalar.activation(log[t // 2][:, t % 2], sig[t // 2][:, t % 2], ACT.Ln, bias=TINY)
            for h in range(HALVES):
                nc.vector.scalar_tensor_tensor(
                    low[h][:, t, :], banks[h, t][:], neg_bias[:, 0, t : t + 1], log[t // 2][:, t % 2, h, :], ALU.add, ALU.min
                )
        for h in range(HALVES):
            with_gain(low[h], 0, h, COLS)

        for h in range(HALVES):
            for t in range(PACK):
                for a in range(PASSES_1):
                    first_product(a, 1, h, [t])
        sig = [slot_tile([P, PACK, COLS], "sig", h) for h in range(HALVES)]
        log = [slot_tile([P, PACK, COLS], "log", 2 + h) for h in range(HALVES)]
        for h in range(HALVES):
            for t in range(PACK):
                nc.scalar.activation(sig[h][:, t, :], banks[h, t][:], ACT.Sigmoid, bias=neg_bias[:, 1, t : t + 1])
        scaled = slot_tile([P, PACK, COLS], "scaled", 10)
        for t in range(PACK):
            nc.vector.tensor_scalar(scaled[:, t, :], banks[0, t][:], neg_bias[:, 1, t : t + 1], gains[:, 1, t : t + 1], ALU.add, ALU.mult)
        tiny = keep.tile([P, 1], F32, name="tiny")
        nc.scalar.activation(tiny[:], sig[1][:, PACK - 1, 0:1], ACT.Identity, scale=0.0, bias=TINY)
        for t in range(PACK):
            nc.scalar.activation(log[0][:, t, :], sig[0][:, t, :], ACT.Ln, bias=tiny[:])
            nc.vector.scalar_tensor_tensor(sig[0][:, t, :], log[0][:, t, :], gains[:, 1, t : t + 1], scaled[:, t, :], ALU.mult, ALU.min)
        grouped = ring.tile([P, PACK * COLS], BF16, name="h_grouped", bufs=3, align_bytes=64)
        nc.vector.tensor_copy(by_runs_out(grouped), by_runs_in(sig[0][:]))
        h_q[1, 0, 0] = quantize(grouped, "h_100")
        for t in range(PACK):
            nc.scalar.activation(log[1][:, t, :], sig[1][:, t, :], ACT.Ln, bias=tiny[:])
            nc.vector.scalar_tensor_tensor(sig[1][:, t, :], banks[1, t][:], neg_bias[:, 1, t : t + 1], log[1][:, t, :], ALU.add, ALU.min)
        with_gain(sig[1], 1, 1, P)

        def second_product(acc, n, b, codes, scales, start, stop):
            nc.tensor.matmul_mx(
                out=acc,
                lhsT=w2_code[:, b, 2 * n * P : 2 * (n + 1) * P].bitcast(FP4X4),
                lhsT_scale=w2_scale[:, b * N + n * P : b * N + (n + 1) * P],
                rhs=codes.bitcast(FP8X4),
                rhs_scale=scales,
                start=start,
                stop=stop,
            )

        for n in range(N // P):
            acc = psum.tile([P, COLS], F32, name=f"bank0{n}")
            for b in range(PASSES_2):
                h_codes, h_scales = h_q[b, 0, 0]
                second_product(acc[:], n, b, h_codes[:], h_scales[:], b == 0, b == 1)
            result = ring.tile([P, COLS], F32, name="result", bufs=8, align_bytes=256)
            nc.scalar.mul(result[:], acc[:], -1.0)
            nc.sync.dma_start(out[n * P : (n + 1) * P, 0:COLS], result[:])
        for c in range(COLS // P):
            last = c == COLS // P - 1
            early = [tile[:, c * P : (c + 1) * P] for tile in h_q[0, 1, 0]]
            late = [tile[:] for tile in h_q[1, 1, c]]
            result = ring.tile([P, COLS], F32, name="result", bufs=8, align_bytes=256)
            if last:
                accs = [psum.tile([P, P], F32, name=f"bank0{n}") for n in range(N // P)]
                for n in range(N // P):
                    second_product(accs[n][:], n, 0, *early, True, False)
                for n in range(N // P):
                    second_product(accs[n][:], n, 1, *late, False, True)
                    if n % 2 == 0:
                        nc.scalar.mul(result[:, n * P : (n + 1) * P], accs[n][:], -1.0)
                    else:
                        nc.vector.tensor_scalar(result[:, n * P : (n + 1) * P], accs[n][:], -1.0, None, ALU.mult)
            else:
                acc = psum.tile([P, COLS], F32, name=f"bank1{c}")
                for n in range(N // P):
                    second_product(acc[:, n * P : (n + 1) * P], n, 0, *early, n == 0, False)
                for n in range(N // P):
                    second_product(acc[:, n * P : (n + 1) * P], n, 1, *late, False, n == N // P - 1)
                nc.scalar.mul(result[:], acc[:], -1.0)
            nc.sync.dma_start(
                out[:, COLS + c * P : COLS + (c + 1) * P].rearrange("(n p) c -> p n c", p=P),
                result[:].rearrange("p (n c) -> p n c", c=P),
            )
